import numpy as np
import ml_dtypes


def mxq(x, axis, fmt="e4m3"):
    dtype, down = {"e4m3": (ml_dtypes.float8_e4m3fn, 7), "e5m2": (ml_dtypes.float8_e5m2, 14)}[fmt]
    v = np.moveaxis(np.asarray(x, np.float32).astype(ml_dtypes.bfloat16).astype(np.float64), axis, -1)
    blocks = v.reshape(v.shape[:-1] + (-1, 32))
    amax = np.abs(blocks).max(-1, keepdims=True)
    byte = np.maximum(np.where(amax > 0, np.frexp(amax)[1] - 1 + 127, 0) - down, 1)
    scale = np.exp2(byte - 127.0)
    codes = (blocks / scale).astype(np.float32).astype(dtype).astype(np.float64)
    return np.moveaxis((codes * scale).reshape(v.shape), -1, axis)


WIDE = False


def mx_kscale(k):
    if not WIDE:
        return np.ones(k)
    levels = np.array([10, -10, 5, -5, 0])
    if k % 512:
        return np.exp2(np.random.permutation(np.resize(levels, k // 32))).repeat(32)
    a = np.empty((k // 512, 16))
    for p in range(k // 512):
        a[p, :8] = np.random.permutation(np.resize(levels, 8))
        for g in range(8):
            far = levels[np.abs(levels - a[p, g]) >= 10]
            a[p, g + 8] = far[np.random.randint(len(far))]
    return np.exp2(a.ravel()).repeat(32)


def f64(x):
    return np.asarray(x).astype(np.float64)


def striped8(idx):
    return np.asarray(idx).reshape(8, -1, 16).transpose(0, 2, 1).reshape(128, -1).astype(np.uint16)


def unstriped8(offs):
    return offs.reshape(8, 16, -1).transpose(0, 2, 1).reshape(8, -1).astype(np.int64)


def pick8(x, idx, run):
    r = np.arange(len(x))
    return x[r[:, None], idx[r % (8 * run) // run]]


E2M1 = np.array([0.0, 0.5, 1.0, 1.5, 2.0, 3.0, 4.0, 6.0, -0.0, -0.5, -1.0, -1.5, -2.0, -3.0, -4.0, -6.0])


def pack_weight(w, fmt):
    k, n = w.shape
    w = f64(np.asarray(w, np.float32).astype(ml_dtypes.bfloat16)).reshape(k // 32, 32, n)
    amax = np.abs(w).max(1)
    if fmt == "e4m3":
        byte = np.frexp(amax)[1] - 1 + 127 - 7
    else:
        mant, ex = np.frexp(amax / 6.0)
        byte = np.where(mant > 0.5, ex, ex - 1) + 127
    byte = np.clip(np.where(amax > 0, byte, 1), 1, 254)
    scaled = (w * np.exp2(127.0 - byte)[:, None, :]).reshape(k, n).astype(np.float32)
    by_word = np.ascontiguousarray(scaled.reshape(k // 512, 128, 4, n).transpose(0, 1, 3, 2))
    if fmt == "e4m3":
        words = by_word.astype(ml_dtypes.float8_e4m3fn).view(np.uint8)
    else:
        c = by_word.astype(ml_dtypes.float4_e2m1fn).view(np.uint8) & 0xF
        words = (c[..., 0::2] | (c[..., 1::2] << 4)).reshape(k // 512, 128, 2 * n)
    return np.ascontiguousarray(words), np.ascontiguousarray(byte.astype(np.uint8).reshape(k // 512, 16, n))


def unpack_weight(words, scales, fmt):
    g, _, n = scales.shape
    words = np.ascontiguousarray(words).reshape(g, 128, n, -1)
    if fmt == "e4m3":
        vals = words.view(ml_dtypes.float8_e4m3fn).astype(np.float64)
    else:
        nib = np.empty((g, 128, n, 4), np.uint8)
        nib[..., 0::2] = words & 0xF
        nib[..., 1::2] = words >> 4
        vals = E2M1[nib]
    vals = vals * np.repeat(np.exp2(scales.astype(np.float64) - 127.0), 8, axis=1)[..., None]
    return vals.transpose(0, 1, 3, 2).reshape(g * 512, n)


D, T, I, Q = 512, 1024, 512, 128


def setup_inputs():
    n = np.random.standard_normal
    idx = np.stack([np.random.permutation(T)[:I] for _ in range(8)])
    idx2 = np.stack([np.random.permutation(T)[:I] for _ in range(8)])
    idx3 = np.stack([np.random.permutation(T)[:I] for _ in range(8)])
    idx4 = np.stack([np.random.permutation(T)[:I] for _ in range(8)])
    fd = mx_kscale(D)
    keysp = pack_weight(n((D, T)) / fd[:, None], "e2m1")
    return {
        "query": (n((D, Q)) * 1.0 / np.sqrt(D) * fd[:, None]).astype(np.float32),
        "keys_words": keysp[0],
        "keys_scales": keysp[1],
        "lam": (np.random.uniform(0.4, 1.0, (Q, 1))).astype(np.float32),
        "old": (1.0 * n((Q, T))).astype(np.float32),
        "offs": striped8(idx),
        "offs2": striped8(idx2),
        "offs3": striped8(idx3),
        "offs4": striped8(idx4),
    }


def reference(query, keys_words, keys_scales, lam, old, offs, offs2, offs3, offs4):
    idx = unstriped8(offs)
    idx2 = unstriped8(offs2)
    idx3 = unstriped8(offs3)
    idx4 = unstriped8(offs4)
    keysu = unpack_weight(keys_words, keys_scales, "e2m1")
    queryq = mxq(f64(query), 0, "e4m3")
    a = queryq.T @ keysu
    w = pick8(a, idx, 16) + np.tanh(pick8(a, idx2, 16) - pick8(a, idx3, 16)) * f64(lam)
    f1 = np.zeros((Q, T))
    f1[np.arange(Q)[:, None], idx4[np.arange(Q) % 128 // 16]] = w
    y = f64(old) + f1
    return y

@@ -1,0 +1,139 @@
+from contextlib import ExitStack
+
+import concourse.mybir as mybir
+
+D, T, SLOTS, Q = 512, 1024, 512, 128
+FLOPS = 2 * D * Q * T
+
+F32 = mybir.dt.float32
+BF16 = mybir.dt.bfloat16
+I32 = mybir.dt.int32
+U32 = mybir.dt.uint32
+U16 = mybir.dt.uint16
+U8 = mybir.dt.uint8
+FP8X4 = mybir.dt.float8_e4m3fn_x4
+FP4X4 = mybir.dt.float4_e2m1fn_x4
+ADD = mybir.AluOpType.add
+SUB = mybir.AluOpType.subtract
+COPY = mybir.ActivationFunctionType.Copy
+TANH = mybir.ActivationFunctionType.Tanh
+
+P = 128
+PACK = 4
+GROUP = 16
+HALF = SLOTS // 2
+PRODUCT_WIDTHS = (256, 256, 256, 128, 128)
+STORE_WIDTH = 256
+
+
+def tile_attend_seconded_lean_putold_heads_kernel(
+    tc, query, keys_words, keys_scales, lam, old, offs, offs2, offs3, offs4, out
+):
+    nc = tc.nc
+    with ExitStack() as ctx:
+        lists = ctx.enter_context(tc.tile_pool(name="lists", bufs=1))
+        keep = ctx.enter_context(tc.tile_pool(name="keep", bufs=1))
+        psum = ctx.enter_context(tc.psum_pool(name="psum", bufs=1))
+
+        key_scales = keep.tile([P, T], U8, align_bytes=64)
+        nc.vector.memset(key_scales[:].bitcast(I32), 0)
+        placed = keep.tile([P, T], F32)
+        nc.vector.memset(placed[:], 0.0)
+
+        query_rows = keep.tile([P, PACK, Q], F32, tag="rows")
+        nc.sync.dma_start(out=query_rows[:], in_=query.rearrange("(p j) q -> p j q", j=PACK))
+        key_words = keep.tile([P, 2 * T], U8, align_bytes=64)
+        nc.sync.dma_start(out=key_words[:].bitcast(I32), in_=keys_words[0].bitcast(I32))
+        for quad in range(4):
+            nc.scalar.dma_start(
+                out=key_scales[32 * quad : 32 * quad + 4, :].bitcast(I32),
+                in_=keys_scales[0, 4 * quad : 4 * quad + 4, :].bitcast(I32),
+            )
+        opponent_list = lists.tile([P, SLOTS // GROUP], U16)
+        nc.sync.dma_start(opponent_list[:], offs3)
+        own_list = lists.tile([P, SLOTS // GROUP], U16)
+        nc.sync.dma_start(own_list[:], offs)
+        seconder_list = lists.tile([P, SLOTS // GROUP], U16)
+        nc.sync.dma_start(seconder_list[:], offs2)
+        place_list = lists.tile([P, SLOTS // GROUP], U16)
+        nc.sync.dma_start(place_list[:], offs4)
+
+        grouped = keep.tile([P, Q, PACK], BF16, tag="grouped", align_bytes=64)
+        nc.vector.tensor_copy(out=grouped[:], in_=query_rows[:].rearrange("p j q -> p q j"))
+        query_codes = keep.tile([P, Q], U32, align_bytes=64)
+        query_scales = keep.tile([P, Q], U8, align_bytes=64)
+        nc.vector.quantize_mx(
+            out=query_codes[:].bitcast(FP8X4),
+            scales=query_scales[:],
+            in_=grouped[:].rearrange("p q j -> p (q j)"),
+        )
+
+        old_rows = keep.tile([P, T], F32, tag="rows")
+        nc.sync.dma_start(out=old_rows[:], in_=old)
+        lam_col = keep.tile([P, 1], F32, tag="grouped", align_bytes=64)
+        nc.sync.dma_start(out=lam_col[:], in_=lam)
+
+        scores = keep.tile([P, T], F32)
+        start = 0
+        for n, width in enumerate(PRODUCT_WIDTHS):
+            bank = psum.tile([P, width], F32, name=f"bank{n}")
+            nc.tensor.matmul_mx(
+                out=bank[:],
+                lhsT=query_codes[:].bitcast(FP8X4),
+                lhsT_scale=query_scales[:],
+                rhs=key_words[:, 2 * start : 2 * (start + width)].bitcast(FP4X4),
+                rhs_scale=key_scales[:, start : start + width],
+                start=True,
+                stop=True,
+            )
+            if n % 2 == 0:
+                nc.scalar.copy(out=scores[:, start : start + width], in_=bank[:])
+            else:
+                nc.vector.tensor_copy(out=scores[:, start : start + width], in_=bank[:])
+            start = start + width
+
+        def half_of(index_list, half):
+            columns = HALF // GROUP
+            return index_list[:, half * columns : (half + 1) * columns]
+
+        quarter = HALF // 2
+        seconder = keep.tile([P, HALF], F32)
+        own_first = keep.tile([P, HALF], F32)
+        nc.vector.tensor_copy(seconder[:], scores[:].indirect(half_of(seconder_list, 0)))
+        nc.vector.tensor_copy(own_first[:], scores[:].indirect(half_of(own_list, 0)))
+        opponents = []
+        for half in range(2):
+            opponent = keep.tile([P, HALF], F32, name=f"opponent{half}")
+            nc.scalar.activation(opponent[:], scores[:].indirect(half_of(opponent_list, half)), COPY)
+            opponents.append(opponent)
+
+        gap_first = keep.tile([P, HALF], F32)
+        staged = keep.tile([P, SLOTS], F32)
+        bent_first = staged[:, quarter : quarter + HALF]
+        lean_first = keep.tile([P, HALF], F32)
+        parts = [slice(0, quarter), slice(quarter, HALF)]
+        for part in parts:
+            nc.vector.tensor_tensor(gap_first[:, part], seconder[:, part], opponents[0][:, part], SUB)
+        for part in parts:
+            nc.scalar.activation(bent_first[:, part], gap_first[:, part], TANH)
+        for part in parts:
+            nc.scalar.activation(lean_first[:, part], bent_first[:, part], COPY, scale=lam_col[:])
+
+        gap_second = keep.tile([P, HALF], F32)
+        nc.vector.tensor_tensor(gap_second[:], scores[:].indirect(half_of(seconder_list, 1)), opponents[1][:], SUB)
+        nc.vector.tensor_tensor(placed[:].indirect(half_of(place_list, 0)), own_first[:], lean_first[:], ADD)
+
+        own_second = staged[:, :HALF]
+        bent_second = staged[:, HALF:]
+        lean_second = keep.tile([P, HALF], F32)
+        nc.scalar.activation(own_second, scores[:].indirect(half_of(own_list, 1)), COPY)
+        nc.scalar.activation(bent_second, gap_second[:], TANH)
+        nc.scalar.activation(lean_second[:], bent_second, COPY, scale=lam_col[:])
+        nc.vector.tensor_tensor(placed[:].indirect(half_of(place_list, 1)), own_second, lean_second[:], ADD)
+
+        total = keep.tile([P, T], F32)
+        for n, start in enumerate(range(0, T, STORE_WIDTH)):
+            cols = slice(start, start + STORE_WIDTH)
+            nc.vector.tensor_tensor(total[:, cols], old_rows[:, cols], placed[:, cols], ADD)
+            queue = nc.sync if n % 2 == 0 else nc.scalar
+            queue.dma_start(out=out[:, cols], in_=total[:, cols])

@@ -59,7 +59,10 @@ def tile_attend_seconded_lean_putold_heads_kernel(
         nc.sync.dma_start(place_list[:], offs4)
 
         grouped = keep.tile([P, Q, PACK], BF16, tag="grouped", align_bytes=64)
-        nc.vector.tensor_copy(out=grouped[:], in_=query_rows[:].rearrange("p j q -> p q j"))
+        nc.vector.tensor_copy(
+            out=grouped[:].rearrange("p (c i) j -> p c j i", i=PACK),
+            in_=query_rows[:].rearrange("p j (c i) -> p c j i", i=PACK),
+        )
         query_codes = keep.tile([P, Q], U32, align_bytes=64)
         query_scales = keep.tile([P, Q], U8, align_bytes=64)
         nc.vector.quantize_mx(
@@ -97,10 +100,10 @@ def tile_attend_seconded_lean_putold_heads_kernel(
             return index_list[:, half * columns : (half + 1) * columns]
 
         quarter = HALF // 2
-        seconder = keep.tile([P, HALF], F32)
-        own_first = keep.tile([P, HALF], F32)
-        nc.vector.tensor_copy(seconder[:], scores[:].indirect(half_of(seconder_list, 0)))
-        nc.vector.tensor_copy(own_first[:], scores[:].indirect(half_of(own_list, 0)))
+        picked = keep.tile([P, SLOTS], F32)
+        seconder = picked[:, quarter : quarter + HALF]
+        own_first = picked[:, :HALF]
+        nc.vector.tensor_copy(seconder, scores[:].indirect(half_of(seconder_list, 0)))
         opponents = []
         for half in range(2):
             opponent = keep.tile([P, HALF], F32, name=f"opponent{half}")
@@ -119,15 +122,16 @@ def tile_attend_seconded_lean_putold_heads_kernel(
         for part in parts:
             nc.scalar.activation(lean_first[:, part], bent_first[:, part], COPY, scale=lam_col[:])
 
-        gap_second = keep.tile([P, HALF], F32)
-        nc.vector.tensor_tensor(gap_second[:], scores[:].indirect(half_of(seconder_list, 1)), opponents[1][:], SUB)
-        nc.vector.tensor_tensor(placed[:].indirect(half_of(place_list, 0)), own_first[:], lean_first[:], ADD)
+        nc.vector.tensor_copy(own_first, scores[:].indirect(half_of(own_list, 0)))
+        gap_second = picked[:, HALF:]
+        nc.vector.tensor_tensor(gap_second, scores[:].indirect(half_of(seconder_list, 1)), opponents[1][:], SUB)
+        nc.vector.tensor_tensor(placed[:].indirect(half_of(place_list, 0)), own_first, lean_first[:], ADD)
 
         own_second = staged[:, :HALF]
         bent_second = staged[:, HALF:]
         lean_second = keep.tile([P, HALF], F32)
         nc.scalar.activation(own_second, scores[:].indirect(half_of(own_list, 1)), COPY)
-        nc.scalar.activation(bent_second, gap_second[:], TANH)
+        nc.scalar.activation(bent_second, gap_second, TANH)
         nc.scalar.activation(lean_second[:], bent_second, COPY, scale=lam_col[:])
         nc.vector.tensor_tensor(placed[:].indirect(half_of(place_list, 1)), own_second, lean_second[:], ADD)
 

from contextlib import ExitStack

import concourse.mybir as mybir

D, T, SLOTS, Q = 512, 1024, 512, 128
FLOPS = 2 * D * Q * T

F32 = mybir.dt.float32
BF16 = mybir.dt.bfloat16
I32 = mybir.dt.int32
U32 = mybir.dt.uint32
U16 = mybir.dt.uint16
U8 = mybir.dt.uint8
FP8X4 = mybir.dt.float8_e4m3fn_x4
FP4X4 = mybir.dt.float4_e2m1fn_x4
ADD = mybir.AluOpType.add
SUB = mybir.AluOpType.subtract
COPY = mybir.ActivationFunctionType.Copy
TANH = mybir.ActivationFunctionType.Tanh

P = 128
PACK = 4
GROUP = 16
HALF = SLOTS // 2
PRODUCT_WIDTHS = (256, 256, 256, 128, 128)
STORE_WIDTH = 256


def tile_attend_seconded_lean_putold_heads_kernel(
    tc, query, keys_words, keys_scales, lam, old, offs, offs2, offs3, offs4, out
):
    nc = tc.nc
    with ExitStack() as ctx:
        lists = ctx.enter_context(tc.tile_pool(name="lists", bufs=1))
        keep = ctx.enter_context(tc.tile_pool(name="keep", bufs=1))
        psum = ctx.enter_context(tc.psum_pool(name="psum", bufs=1))

        key_scales = keep.tile([P, T], U8, align_bytes=64)
        nc.vector.memset(key_scales[:].bitcast(I32), 0)
        placed = keep.tile([P, T], F32)
        nc.vector.memset(placed[:], 0.0)

        query_rows = keep.tile([P, PACK, Q], F32, tag="rows")
        nc.sync.dma_start(out=query_rows[:], in_=query.rearrange("(p j) q -> p j q", j=PACK))
        key_words = keep.tile([P, 2 * T], U8, align_bytes=64)
        nc.sync.dma_start(out=key_words[:].bitcast(I32), in_=keys_words[0].bitcast(I32))
        for quad in range(4):
            nc.scalar.dma_start(
                out=key_scales[32 * quad : 32 * quad + 4, :].bitcast(I32),
                in_=keys_scales[0, 4 * quad : 4 * quad + 4, :].bitcast(I32),
            )
        opponent_list = lists.tile([P, SLOTS // GROUP], U16)
        nc.sync.dma_start(opponent_list[:], offs3)
        own_list = lists.tile([P, SLOTS // GROUP], U16)
        nc.sync.dma_start(own_list[:], offs)
        seconder_list = lists.tile([P, SLOTS // GROUP], U16)
        nc.sync.dma_start(seconder_list[:], offs2)
        place_list = lists.tile([P, SLOTS // GROUP], U16)
        nc.sync.dma_start(place_list[:], offs4)

        grouped = keep.tile([P, Q, PACK], BF16, tag="grouped", align_bytes=64)
        nc.vector.tensor_copy(
            out=grouped[:].rearrange("p (c i) j -> p c j i", i=PACK),
            in_=query_rows[:].rearrange("p j (c i) -> p c j i", i=PACK),
        )
        query_codes = keep.tile([P, Q], U32, align_bytes=64)
        query_scales = keep.tile([P, Q], U8, align_bytes=64)
        nc.vector.quantize_mx(
            out=query_codes[:].bitcast(FP8X4),
            scales=query_scales[:],
            in_=grouped[:].rearrange("p q j -> p (q j)"),
        )

        old_rows = keep.tile([P, T], F32, tag="rows")
        nc.sync.dma_start(out=old_rows[:], in_=old)
        lam_col = keep.tile([P, 1], F32, tag="grouped", align_bytes=64)
        nc.sync.dma_start(out=lam_col[:], in_=lam)

        scores = keep.tile([P, T], F32)
        start = 0
        for n, width in enumerate(PRODUCT_WIDTHS):
            bank = psum.tile([P, width], F32, name=f"bank{n}")
            nc.tensor.matmul_mx(
                out=bank[:],
                lhsT=query_codes[:].bitcast(FP8X4),
                lhsT_scale=query_scales[:],
                rhs=key_words[:, 2 * start : 2 * (start + width)].bitcast(FP4X4),
                rhs_scale=key_scales[:, start : start + width],
                start=True,
                stop=True,
            )
            if n % 2 == 0:
                nc.scalar.copy(out=scores[:, start : start + width], in_=bank[:])
            else:
                nc.vector.tensor_copy(out=scores[:, start : start + width], in_=bank[:])
            start = start + width

        def half_of(index_list, half):
            columns = HALF // GROUP
            return index_list[:, half * columns : (half + 1) * columns]

        quarter = HALF // 2
        picked = keep.tile([P, SLOTS], F32)
        seconder = picked[:, quarter : quarter + HALF]
        own_first = picked[:, :HALF]
        nc.vector.tensor_copy(seconder, scores[:].indirect(half_of(seconder_list, 0)))
        opponents = []
        for half in range(2):
            opponent = keep.tile([P, HALF], F32, name=f"opponent{half}")
            nc.scalar.activation(opponent[:], scores[:].indirect(half_of(opponent_list, half)), COPY)
            opponents.append(opponent)

        gap_first = keep.tile([P, HALF], F32)
        staged = keep.tile([P, SLOTS], F32)
        bent_first = staged[:, quarter : quarter + HALF]
        lean_first = keep.tile([P, HALF], F32)
        parts = [slice(0, quarter), slice(quarter, HALF)]
        for part in parts:
            nc.vector.tensor_tensor(gap_first[:, part], seconder[:, part], opponents[0][:, part], SUB)
        for part in parts:
            nc.scalar.activation(bent_first[:, part], gap_first[:, part], TANH)
        for part in parts:
            nc.scalar.activation(lean_first[:, part], bent_first[:, part], COPY, scale=lam_col[:])

        nc.vector.tensor_copy(own_first, scores[:].indirect(half_of(own_list, 0)))
        gap_second = picked[:, HALF:]
        nc.vector.tensor_tensor(gap_second, scores[:].indirect(half_of(seconder_list, 1)), opponents[1][:], SUB)
        nc.vector.tensor_tensor(placed[:].indirect(half_of(place_list, 0)), own_first, lean_first[:], ADD)

        own_second = staged[:, :HALF]
        bent_second = staged[:, HALF:]
        lean_second = keep.tile([P, HALF], F32)
        nc.scalar.activation(own_second, scores[:].indirect(half_of(own_list, 1)), COPY)
        nc.scalar.activation(bent_second, gap_second, TANH)
        nc.scalar.activation(lean_second[:], bent_second, COPY, scale=lam_col[:])
        nc.vector.tensor_tensor(placed[:].indirect(half_of(place_list, 1)), own_second, lean_second[:], ADD)

        total = keep.tile([P, T], F32)
        for n, start in enumerate(range(0, T, STORE_WIDTH)):
            cols = slice(start, start + STORE_WIDTH)
            nc.vector.tensor_tensor(total[:, cols], old_rows[:, cols], placed[:, cols], ADD)
            queue = nc.sync if n % 2 == 0 else nc.scalar
            queue.dma_start(out=out[:, cols], in_=total[:, cols])
